import numpy as np
import ml_dtypes


def mxq(x, axis, fmt="e4m3"):
    dtype, down = {"e4m3": (ml_dtypes.float8_e4m3fn, 7), "e5m2": (ml_dtypes.float8_e5m2, 14)}[fmt]
    v = np.moveaxis(np.asarray(x, np.float32).astype(ml_dtypes.bfloat16).astype(np.float64), axis, -1)
    blocks = v.reshape(v.shape[:-1] + (-1, 32))
    amax = np.abs(blocks).max(-1, keepdims=True)
    byte = np.maximum(np.where(amax > 0, np.frexp(amax)[1] - 1 + 127, 0) - down, 1)
    scale = np.exp2(byte - 127.0)
    codes = (blocks / scale).astype(np.float32).astype(dtype).astype(np.float64)
    return np.moveaxis((codes * scale).reshape(v.shape), -1, axis)


WIDE = False


def mx_kscale(k):
    if not WIDE:
        return np.ones(k)
    levels = np.array([30, -30])
    if k % 512:
        return np.exp2(np.random.permutation(np.resize(levels, k // 32))).repeat(32)
    a = np.empty((k // 512, 16))
    for p in range(k // 512):
        a[p, :8] = np.random.permutation(np.resize(levels, 8))
        for g in range(8):
            far = levels[np.abs(levels - a[p, g]) >= 10]
            a[p, g + 8] = far[np.random.randint(len(far))]
    return np.exp2(a.ravel()).repeat(32)


def f64(x):
    return np.asarray(x).astype(np.float64)


def striped(idx):
    return np.tile(np.asarray(idx).reshape(-1, 16).T, (8, 1)).astype(np.uint16)


def unstriped(offs):
    return offs[:16].T.reshape(-1).astype(np.int64)


def striped8(idx):
    return np.asarray(idx).reshape(8, -1, 16).transpose(0, 2, 1).reshape(128, -1).astype(np.uint16)


def unstriped8(offs):
    return offs.reshape(8, 16, -1).transpose(0, 2, 1).reshape(8, -1).astype(np.int64)


def pick8(x, idx, run):
    r = np.arange(len(x))
    return x[r[:, None], idx[r % (8 * run) // run]]


E2M1 = np.array([0.0, 0.5, 1.0, 1.5, 2.0, 3.0, 4.0, 6.0, -0.0, -0.5, -1.0, -1.5, -2.0, -3.0, -4.0, -6.0])


def pack_weight(w, fmt):
    k, n = w.shape
    w = f64(np.asarray(w, np.float32).astype(ml_dtypes.bfloat16)).reshape(k // 32, 32, n)
    amax = np.abs(w).max(1)
    if fmt in ("e4m3", "e5m2"):
        byte = np.frexp(amax)[1] - 1 + 127 - (7 if fmt == "e4m3" else 14)
    else:
        mant, ex = np.frexp(amax / 6.0)
        byte = np.where(mant > 0.5, ex, ex - 1) + 127
    byte = np.clip(np.where(amax > 0, byte, 1), 1, 254)
    scaled = (w * np.exp2(127.0 - byte)[:, None, :]).reshape(k, n).astype(np.float32)
    by_word = np.ascontiguousarray(scaled.reshape(k // 512, 128, 4, n).transpose(0, 1, 3, 2))
    if fmt in ("e4m3", "e5m2"):
        words = by_word.astype(ml_dtypes.float8_e4m3fn if fmt == "e4m3" else ml_dtypes.float8_e5m2).view(np.uint8)
    else:
        c = by_word.astype(ml_dtypes.float4_e2m1fn).view(np.uint8) & 0xF
        words = (c[..., 0::2] | (c[..., 1::2] << 4)).reshape(k // 512, 128, 2 * n)
    return np.ascontiguousarray(words), np.ascontiguousarray(byte.astype(np.uint8).reshape(k // 512, 16, n))


def unpack_weight(words, scales, fmt):
    g, _, n = scales.shape
    words = np.ascontiguousarray(words).reshape(g, 128, n, -1)
    if fmt in ("e4m3", "e5m2"):
        vals = words.view(ml_dtypes.float8_e4m3fn if fmt == "e4m3" else ml_dtypes.float8_e5m2).astype(np.float64)
    else:
        nib = np.empty((g, 128, n, 4), np.uint8)
        nib[..., 0::2] = words & 0xF
        nib[..., 1::2] = words >> 4
        vals = E2M1[nib]
    vals = vals * np.repeat(np.exp2(scales.astype(np.float64) - 127.0), 8, axis=1)[..., None]
    return vals.transpose(0, 1, 3, 2).reshape(g * 512, n)


K, T, J, R, F, Z, C, N, U = 512, 1024, 256, 512, 512, 1024, 512, 256, 256


def setup_inputs():
    n = np.random.standard_normal
    idx = np.random.permutation(T)[:J]
    idx2 = np.random.permutation(Z)[:J]
    idx3 = np.stack([np.random.permutation(C)[:J] for _ in range(8)])
    idx4 = np.stack([np.random.permutation(C)[:J] for _ in range(8)])
    idx5 = np.random.permutation(C)[:U]
    idx6 = np.random.permutation(C)[:U]
    fk = mx_kscale(K)
    ff = mx_kscale(F)
    fr = mx_kscale(R)
    xtp = pack_weight(n((K, T)) / fk[:, None], "e2m1")
    xop = pack_weight(n((F, Z)) / ff[:, None], "e5m2")
    wp = pack_weight(n((K, R)) * 1 / np.sqrt(K) * fk[:, None] * fr, "e5m2")
    w2p = pack_weight(n((F, R)) * 1 / np.sqrt(F) * ff[:, None] * fr, "e4m3")
    wbp = pack_weight(n((R, N)) * 1 / np.sqrt(R) / fr[:, None], "e4m3")
    wcp = pack_weight(n((R, N)) * 1 / np.sqrt(R) / fr[:, None], "e2m1")
    return {
        "xt_words": xtp[0],
        "xt_scales": xtp[1],
        "xo_words": xop[0],
        "xo_scales": xop[1],
        "w_words": wp[0],
        "w_scales": wp[1],
        "w2_words": w2p[0],
        "w2_scales": w2p[1],
        "wb_words": wbp[0],
        "wb_scales": wbp[1],
        "wc_words": wcp[0],
        "wc_scales": wcp[1],
        "so": (np.random.uniform(0.5, 1.6, (N, 1))).astype(np.float32),
        "offs": striped(idx),
        "offs2": striped(idx2),
        "offs3": striped8(idx3),
        "offs4": striped8(idx4),
        "offs5": striped(idx5),
        "offs6": striped(idx6),
    }


def reference(xt_words, xt_scales, xo_words, xo_scales, w_words, w_scales, w2_words, w2_scales, wb_words, wb_scales, wc_words, wc_scales, so, offs, offs2, offs3, offs4, offs5, offs6):
    idx = unstriped(offs)
    idx2 = unstriped(offs2)
    idx3 = unstriped8(offs3)
    idx4 = unstriped8(offs4)
    idx5 = unstriped(offs5)
    idx6 = unstriped(offs6)
    xtu = unpack_weight(xt_words, xt_scales, "e2m1")
    xou = unpack_weight(xo_words, xo_scales, "e5m2")
    wu = unpack_weight(w_words, w_scales, "e5m2")
    w2u = unpack_weight(w2_words, w2_scales, "e4m3")
    wbu = unpack_weight(wb_words, wb_scales, "e4m3")
    wcu = unpack_weight(wc_words, wc_scales, "e2m1")
    xtidxg = xtu[:, idx]
    a = wu.T @ xtidxg
    xoidx2g = xou[:, idx2]
    b = w2u.T @ xoidx2g
    pa = np.zeros((R, C))
    pa[np.arange(R)[:, None], idx3[np.arange(R) % 512 // 64]] = a
    pb = np.zeros((R, C))
    pb[np.arange(R)[:, None], idx4[np.arange(R) % 512 // 64]] = b
    paq = mxq(pa, 0, "e4m3")
    pbq = mxq(pb, 0, "e4m3")
    p = wbu.T @ paq + wcu.T @ pbq
    y = np.maximum(p[:, idx5] * f64(so), p[:, idx6])
    return y

@@ -1,0 +1,236 @@
+from contextlib import ExitStack
+
+import concourse.mybir as mybir
+
+K, T, J, R, F, Z, C, N, U = 512, 1024, 256, 512, 512, 1024, 512, 256, 256
+FLOPS = 2 * K * R * J + 2 * F * R * J + 2 * 2 * R * N * C
+
+F32 = mybir.dt.float32
+BF16 = mybir.dt.bfloat16
+I32 = mybir.dt.int32
+U32 = mybir.dt.uint32
+U16 = mybir.dt.uint16
+U8 = mybir.dt.uint8
+E4M3 = mybir.dt.float8_e4m3fn_x4
+E5M2 = mybir.dt.float8_e5m2_x4
+E2M1 = mybir.dt.float4_e2m1fn_x4
+COPY = mybir.ActivationFunctionType.Copy
+MAX = mybir.AluOpType.max
+
+P = 128
+PACK = 4
+QUADS = 4
+HALF_J = J // 2
+HALF_C = C // 2
+LIST_COLS = J // 16
+
+
+def tile_list_boardssum_kernel(tc, xt_words, xt_scales, xo_words, xo_scales, w_words, w_scales,
+                                     w2_words, w2_scales, wb_words, wb_scales, wc_words, wc_scales,
+                                     so, offs, offs2, offs3, offs4, offs5, offs6, out):
+    nc = tc.nc
+    with ExitStack() as ctx:
+        sb = ctx.enter_context(tc.tile_pool(name="sb", bufs=1))
+        ps = ctx.enter_context(tc.psum_pool(name="ps", bufs=1))
+
+        def tile(name, shape, dtype, tag=None):
+            return sb.tile(shape, dtype, name=name, tag=tag or name, align_bytes=64)
+
+        def load_list(name, src):
+            t = sb.tile([P, LIST_COLS], U16, name=name)
+            nc.sync.dma_start(t[:], src)
+            return t
+
+        def words_i32(src):
+            return src[0].rearrange("p n t -> p (n t)").bitcast(I32)
+
+        def stage_scales(name, src, width):
+            t = tile(name, [QUADS, QUADS, width // 4], I32)
+            nc.sync.dma_start(t[:], src[0].bitcast(I32).rearrange("(q r) c -> r q c", q=QUADS))
+            return t
+
+        def spread_scales(plane, staged):
+            for q in range(QUADS):
+                nc.vector.tensor_copy(plane[32 * q : 32 * q + QUADS, :].bitcast(I32), staged[:, q, :])
+
+        def load_scales(plane, src):
+            for q in range(QUADS):
+                nc.sync.dma_start(plane[32 * q : 32 * q + QUADS, :].bitcast(I32),
+                                  src[0, QUADS * q : QUADS * (q + 1), :].bitcast(I32))
+
+        def zero_plane(name, width):
+            t = tile(name, [P, width], U8)
+            nc.vector.memset(t[:].bitcast(I32), 0)
+            return t
+
+        def zero_board(engine, name, tag=None):
+            t = tile(name, [P, C], F32, tag=tag)
+            engine.memset(t[:], 0.0)
+            return t
+
+        def deal_words(dst, src, t0, t1):
+            nc.vector.tensor_copy(dst[:].rearrange("p (t m) -> p m t", t=PACK)[:, :, t0:t1],
+                                  src[:].rearrange("p (m t) -> p m t", t=PACK)[:, :, t0:t1])
+
+        def deal_scales(engine, dst, src, t0, t1):
+            engine.tensor_copy(dst[:].rearrange("p (t m) -> p t m", t=PACK)[:, t0:t1, :],
+                               src[:].rearrange("p (m t) -> p t m", t=PACK)[:, t0:t1, :])
+
+        l1 = load_list("l1", offs)
+        xt_stage = stage_scales("xt_stage", xt_scales, T)
+        w_stage = stage_scales("w_stage", w_scales, R)
+        l3 = load_list("l3", offs3)
+        xt_w = tile("xt_w", [P, T], U16)
+        nc.scalar.dma_start(xt_w[:].bitcast(I32), xt_words[0].bitcast(I32))
+        w_raw = tile("w_raw", [P, R], U32)
+        nc.scalar.dma_start(w_raw[:].bitcast(I32), words_i32(w_words))
+        l2 = load_list("l2", offs2)
+        xo_w = tile("xo_w", [P, Z], U32)
+        nc.sync.dma_start(xo_w[:].bitcast(I32), words_i32(xo_words))
+        w2_raw = tile("w2_raw", [P, R], U32)
+        nc.sync.dma_start(w2_raw[:].bitcast(I32), words_i32(w2_words))
+
+        xt_s = zero_plane("xt_s", T)
+        w_s_raw = zero_plane("w_s_raw", R)
+        xo_s = zero_plane("xo_s", Z)
+        w2_s_raw = zero_plane("w2_s_raw", R)
+        wb_s = zero_plane("wb_s", N)
+        wc_s = zero_plane("wc_s", N)
+        board_a = [zero_board(nc.vector, f"board_a{t}") for t in range(PACK)]
+
+        load_scales(xo_s, xo_scales)
+        load_scales(w2_s_raw, w2_scales)
+        l4 = load_list("l4", offs4)
+        wb_w = tile("wb_w", [P, N], U32)
+        nc.sync.dma_start(wb_w[:].bitcast(I32), words_i32(wb_words))
+        load_scales(wb_s, wb_scales)
+        wc_w = tile("wc_w", [P, 2 * N], U8)
+        nc.sync.dma_start(wc_w[:].bitcast(I32), wc_words[0].bitcast(I32))
+        load_scales(wc_s, wc_scales)
+        l5 = load_list("l5", offs5)
+        l6 = load_list("l6", offs6)
+        so_t = tile("so_t", [P, N // P], F32)
+        with nc.allow_non_contiguous_dma(reason="one weight a partition"):
+            nc.sync.dma_start(so_t[:], so.rearrange("(s p) o -> p (s o)", p=P))
+
+        spread_scales(w_s_raw, w_stage)
+        spread_scales(xt_s, xt_stage)
+        w_s = tile("w_s", [P, R], U8)
+        w_w = tile("w_w", [P, R], U32)
+        deal_scales(nc.vector, w_s, w_s_raw, 0, 1)
+        deal_words(w_w, w_raw, 0, 1)
+
+        xg_w, xg_s = [], []
+
+        def gather_xt(h):
+            cols = slice(h * LIST_COLS // 2, (h + 1) * LIST_COLS // 2)
+            gw = tile(f"xg_w{h}", [P, HALF_J], U16)
+            nc.vector.tensor_copy(gw[:], xt_w[:].indirect(l1[:, cols]))
+            gs = tile(f"xg_s{h}", [P, HALF_J], U8)
+            nc.vector.tensor_copy(gs[:], xt_s[:].indirect(l1[:, cols]))
+            xg_w.append(gw)
+            xg_s.append(gs)
+
+        gather_xt(0)
+        deal_scales(nc.vector, w_s, w_s_raw, 1, PACK)
+        deal_words(w_w, w_raw, 1, PACK)
+
+        def product_a(dst, t, h):
+            cols = slice(t * P, (t + 1) * P)
+            nc.tensor.matmul_mx(dst, lhsT=w_w[:, cols].bitcast(E5M2), lhsT_scale=w_s[:, cols],
+                                rhs=xg_w[h][:].bitcast(E2M1), rhs_scale=xg_s[h][:], start=True, stop=True)
+
+        a_src = {}
+
+        def products_a(h, t0, t1, bank, on_scalar=False):
+            acc = ps.tile([P, t1 - t0, HALF_J], F32, name=f"a_ps{h}{t0}", tag=f"bank{bank}")
+            for t in range(t0, t1):
+                product_a(acc[:, t - t0, :], t, h)
+            staged = tile(f"a_sb{h}{t0}", [P, t1 - t0, HALF_J], F32)
+            if on_scalar:
+                nc.scalar.activation(staged[:], acc[:], COPY)
+            else:
+                nc.vector.tensor_copy(staged[:], acc[:])
+            for t in range(t0, t1):
+                a_src[(h, t)] = staged[:, t - t0, :]
+
+        products_a(0, 0, 1, 0, on_scalar=True)
+        products_a(0, 1, 2, 5)
+        products_a(0, 2, 4, 1)
+        gather_xt(1)
+        products_a(1, 0, 2, 2)
+        products_a(1, 2, 4, 6)
+        for h in range(2):
+            cols = slice(h * LIST_COLS // 2, (h + 1) * LIST_COLS // 2)
+            for t in range(PACK):
+                nc.scalar.activation(board_a[t][:].indirect(l3[:, cols]), a_src[(h, t)], COPY)
+
+        board_b = [zero_board(nc.gpsimd, f"board_b{t}", tag=old) for t, old in enumerate(["xg_w0", "xg_s0", "xg_w1", "xg_s1"])]
+        w2_s = tile("w2_s", [P, R], U8, tag="w_s")
+        deal_scales(nc.gpsimd, w2_s, w2_s_raw, 0, PACK)
+        og_w = tile("og_w", [P, J], U32, tag="xt_w")
+        nc.vector.tensor_copy(og_w[:], xo_w[:].indirect(l2[:]))
+        og_s = tile("og_s", [P, J], U8, tag="xt_s")
+        nc.vector.tensor_copy(og_s[:], xo_s[:].indirect(l2[:]))
+        w2_w = tile("w2_w", [P, R], U32, tag="w_w")
+        deal_words(w2_w, w2_raw, 0, PACK)
+        b_sb = []
+        for pair in range(2):
+            bank = ps.tile([P, 2, J], F32, name=f"b_ps{pair}", tag=f"bank{3 + pair}")
+            for e in range(2):
+                cols = slice((2 * pair + e) * P, (2 * pair + e + 1) * P)
+                nc.tensor.matmul_mx(bank[:, e, :], lhsT=w2_w[:, cols].bitcast(E4M3), lhsT_scale=w2_s[:, cols],
+                                    rhs=og_w[:].bitcast(E5M2), rhs_scale=og_s[:], start=True, stop=True)
+            staged = tile(f"b_sb{pair}", [P, 2, J], F32)
+            nc.vector.tensor_copy(staged[:], bank[:])
+            b_sb.append(staged)
+        for t in range(PACK):
+            nc.scalar.activation(board_b[t][:].indirect(l4[:]), b_sb[t // 2][:, t % 2, :], COPY)
+
+        a_planes = tile("a_planes", [P, PACK, C], BF16, tag="w_w")
+        for t in range(PACK):
+            nc.vector.tensor_copy(a_planes[:, t, :], board_a[t][:])
+        a_woven = tile("a_woven", [P, C, PACK], BF16)
+        nc.vector.tensor_copy(a_woven[:].rearrange("p (c i) t -> p c t i", i=4),
+                              a_planes[:].rearrange("p t (c i) -> p c t i", i=4))
+        pa_w = tile("pa_w", [P, C], U32)
+        pa_s = tile("pa_s", [P, C], U8)
+        nc.vector.quantize_mx(out=pa_w[:].bitcast(E4M3), scales=pa_s[:], in_=a_woven[:].rearrange("p c t -> p (c t)"))
+        sums = {}
+        for k, (h, s) in enumerate([(h, s) for h in range(2) for s in range(2)]):
+            bank = ps.tile([P, HALF_C], F32, name=f"p_ps{h}{s}", tag=f"bank{(5 + k) % 8}")
+            ncols = slice(s * P, (s + 1) * P)
+            ccols = slice(h * HALF_C, (h + 1) * HALF_C)
+            nc.tensor.matmul_mx(bank[:], lhsT=wb_w[:, ncols].bitcast(E4M3), lhsT_scale=wb_s[:, ncols],
+                                rhs=pa_w[:, ccols].bitcast(E4M3), rhs_scale=pa_s[:, ccols], start=True, stop=False)
+            sums[(h, s)] = bank
+
+        b_woven = [tile(f"b_woven{h}", [P, HALF_C, PACK], BF16) for h in range(2)]
+        for t in range(PACK):
+            for h in range(2):
+                nc.vector.tensor_copy(b_woven[h][:, :, t], board_b[t][:, h * HALF_C : (h + 1) * HALF_C])
+        p_sb = [tile(f"p_sb{s}", [P, C], F32) for s in range(2)]
+        for h in range(2):
+            pb_w = tile(f"pb_w{h}", [P, HALF_C], U32)
+            pb_s = tile(f"pb_s{h}", [P, HALF_C], U8)
+            nc.vector.quantize_mx(out=pb_w[:].bitcast(E4M3), scales=pb_s[:], in_=b_woven[h][:].rearrange("p c t -> p (c t)"))
+            for s in range(2):
+                nc.tensor.matmul_mx(sums[(h, s)][:], lhsT=wc_w[:, 2 * s * P : 2 * (s + 1) * P].bitcast(E2M1),
+                                    lhsT_scale=wc_s[:, s * P : (s + 1) * P],
+                                    rhs=pb_w[:].bitcast(E4M3), rhs_scale=pb_s[:], start=False, stop=True)
+        for h in range(2):
+            for s in range(2):
+                dst = p_sb[s][:, h * HALF_C : (h + 1) * HALF_C]
+                if (h, s) == (1, 1):
+                    nc.vector.tensor_copy(dst, sums[(h, s)][:])
+                else:
+                    nc.scalar.copy(dst, sums[(h, s)][:])
+
+        for s in range(2):
+            scaled = tile(f"scaled{s}", [P, U], F32)
+            nc.scalar.activation(scaled[:], p_sb[s][:].indirect(l5[:]), COPY, scale=so_t[:, s : s + 1])
+            picked = tile(f"picked{s}", [P, U], F32)
+            nc.vector.tensor_copy(picked[:], p_sb[s][:].indirect(l6[:]))
+            best = tile(f"best{s}", [P, U], F32)
+            nc.vector.tensor_tensor(best[:], scaled[:], picked[:], MAX)
+            nc.sync.dma_start(out[s * P : (s + 1) * P, :], best[:])

@@ -22,6 +22,7 @@ PACK = 4
 QUADS = 4
 HALF_J = J // 2
 HALF_C = C // 2
+QUART_C = C // 4
 LIST_COLS = J // 16
 
 
@@ -45,13 +46,16 @@ def tile_list_boardssum_kernel(tc, xt_words, xt_scales, xo_words, xo_scales, w_w
             return src[0].rearrange("p n t -> p (n t)").bitcast(I32)
 
         def stage_scales(name, src, width):
-            t = tile(name, [QUADS, QUADS, width // 4], I32)
-            nc.sync.dma_start(t[:], src[0].bitcast(I32).rearrange("(q r) c -> r q c", q=QUADS))
+            t = tile(name, [P, 2, width // 4], I32)
+            rows = src[0].bitcast(I32).rearrange("(g q r) c -> g r q c", g=2, q=2)
+            nc.sync.dma_start(t[0:QUADS, :, :], rows[0])
+            nc.scalar.dma_start(t[64 : 64 + QUADS, :, :], rows[1])
             return t
 
         def spread_scales(plane, staged):
             for q in range(QUADS):
-                nc.vector.tensor_copy(plane[32 * q : 32 * q + QUADS, :].bitcast(I32), staged[:, q, :])
+                first = 64 * (q // 2)
+                nc.vector.tensor_copy(plane[32 * q : 32 * q + QUADS, :].bitcast(I32), staged[first : first + QUADS, q % 2, :])
 
         def load_scales(plane, src):
             for q in range(QUADS):
@@ -79,11 +83,11 @@ def tile_list_boardssum_kernel(tc, xt_words, xt_scales, xo_words, xo_scales, w_w
         l1 = load_list("l1", offs)
         xt_stage = stage_scales("xt_stage", xt_scales, T)
         w_stage = stage_scales("w_stage", w_scales, R)
-        l3 = load_list("l3", offs3)
         xt_w = tile("xt_w", [P, T], U16)
-        nc.scalar.dma_start(xt_w[:].bitcast(I32), xt_words[0].bitcast(I32))
+        nc.sync.dma_start(xt_w[:].bitcast(I32), xt_words[0].bitcast(I32))
         w_raw = tile("w_raw", [P, R], U32)
-        nc.scalar.dma_start(w_raw[:].bitcast(I32), words_i32(w_words))
+        nc.sync.dma_start(w_raw[:].bitcast(I32), words_i32(w_words))
+        l3 = load_list("l3", offs3)
         l2 = load_list("l2", offs2)
         xo_w = tile("xo_w", [P, Z], U32)
         nc.sync.dma_start(xo_w[:].bitcast(I32), words_i32(xo_words))
@@ -96,7 +100,7 @@ def tile_list_boardssum_kernel(tc, xt_words, xt_scales, xo_words, xo_scales, w_w
         w2_s_raw = zero_plane("w2_s_raw", R)
         wb_s = zero_plane("wb_s", N)
         wc_s = zero_plane("wc_s", N)
-        board_a = [zero_board(nc.vector, f"board_a{t}") for t in range(PACK)]
+        board_a = [zero_board(nc.vector if t < 2 else nc.gpsimd, f"board_a{t}") for t in range(PACK)]
 
         load_scales(xo_s, xo_scales)
         load_scales(w2_s_raw, w2_scales)
@@ -113,59 +117,45 @@ def tile_list_boardssum_kernel(tc, xt_words, xt_scales, xo_words, xo_scales, w_w
         with nc.allow_non_contiguous_dma(reason="one weight a partition"):
             nc.sync.dma_start(so_t[:], so.rearrange("(s p) o -> p (s o)", p=P))
 
-        spread_scales(w_s_raw, w_stage)
         spread_scales(xt_s, xt_stage)
+        spread_scales(w_s_raw, w_stage)
         w_s = tile("w_s", [P, R], U8)
         w_w = tile("w_w", [P, R], U32)
+        xg_w = tile("xg_w", [P, J], U16)
+        xg_s = tile("xg_s", [P, J], U8)
+
+        def gather_xt(j0, j1):
+            nc.vector.tensor_copy(xg_s[:, j0:j1], xt_s[:].indirect(l1[:, j0 // 16 : j1 // 16]))
+            nc.vector.tensor_copy(xg_w[:, j0:j1], xt_w[:].indirect(l1[:, j0 // 16 : j1 // 16]))
+
         deal_scales(nc.vector, w_s, w_s_raw, 0, 1)
+        gather_xt(0, HALF_J)
         deal_words(w_w, w_raw, 0, 1)
-
-        xg_w, xg_s = [], []
-
-        def gather_xt(h):
-            cols = slice(h * LIST_COLS // 2, (h + 1) * LIST_COLS // 2)
-            gw = tile(f"xg_w{h}", [P, HALF_J], U16)
-            nc.vector.tensor_copy(gw[:], xt_w[:].indirect(l1[:, cols]))
-            gs = tile(f"xg_s{h}", [P, HALF_J], U8)
-            nc.vector.tensor_copy(gs[:], xt_s[:].indirect(l1[:, cols]))
-            xg_w.append(gw)
-            xg_s.append(gs)
-
-        gather_xt(0)
         deal_scales(nc.vector, w_s, w_s_raw, 1, PACK)
         deal_words(w_w, w_raw, 1, PACK)
 
-        def product_a(dst, t, h):
-            cols = slice(t * P, (t + 1) * P)
-            nc.tensor.matmul_mx(dst, lhsT=w_w[:, cols].bitcast(E5M2), lhsT_scale=w_s[:, cols],
-                                rhs=xg_w[h][:].bitcast(E2M1), rhs_scale=xg_s[h][:], start=True, stop=True)
-
-        a_src = {}
-
-        def products_a(h, t0, t1, bank, on_scalar=False):
-            acc = ps.tile([P, t1 - t0, HALF_J], F32, name=f"a_ps{h}{t0}", tag=f"bank{bank}")
-            for t in range(t0, t1):
-                product_a(acc[:, t - t0, :], t, h)
-            staged = tile(f"a_sb{h}{t0}", [P, t1 - t0, HALF_J], F32)
+        def products_a(ts, j0, j1, bank, on_scalar=False):
+            acc = ps.tile([P, len(ts), j1 - j0], F32, name=f"a_ps{bank}", tag=f"bank{bank}")
+            for e, t in enumerate(ts):
+                cols = slice(t * P, (t + 1) * P)
+                nc.tensor.matmul_mx(acc[:, e, :], lhsT=w_w[:, cols].bitcast(E5M2), lhsT_scale=w_s[:, cols],
+                                    rhs=xg_w[:, j0:j1].bitcast(E2M1), rhs_scale=xg_s[:, j0:j1], start=True, stop=True)
+            staged = tile(f"a_sb{bank}", [P, len(ts), j1 - j0], F32)
             if on_scalar:
                 nc.scalar.activation(staged[:], acc[:], COPY)
             else:
                 nc.vector.tensor_copy(staged[:], acc[:])
-            for t in range(t0, t1):
-                a_src[(h, t)] = staged[:, t - t0, :]
+            for e, t in enumerate(ts):
+                nc.scalar.activation(board_a[t][:].indirect(l3[:, j0 // 16 : j1 // 16]), staged[:, e, :], COPY)
 
-        products_a(0, 0, 1, 0, on_scalar=True)
-        products_a(0, 1, 2, 5)
-        products_a(0, 2, 4, 1)
-        gather_xt(1)
-        products_a(1, 0, 2, 2)
-        products_a(1, 2, 4, 6)
-        for h in range(2):
-            cols = slice(h * LIST_COLS // 2, (h + 1) * LIST_COLS // 2)
-            for t in range(PACK):
-                nc.scalar.activation(board_a[t][:].indirect(l3[:, cols]), a_src[(h, t)], COPY)
+        products_a([0], 0, HALF_J, 0, on_scalar=True)
+        products_a([1], 0, HALF_J, 5)
+        gather_xt(HALF_J, J)
+        products_a([2], 0, J, 1)
+        products_a([3], 0, J, 2)
+        products_a([0, 1], HALF_J, J, 6)
 
-        board_b = [zero_board(nc.gpsimd, f"board_b{t}", tag=old) for t, old in enumerate(["xg_w0", "xg_s0", "xg_w1", "xg_s1"])]
+        board_b = [zero_board(nc.gpsimd, f"board_b{t}", tag=old) for t, old in enumerate(["w_raw", "w_s_raw", "xg_w", "xg_s"])]
         w2_s = tile("w2_s", [P, R], U8, tag="w_s")
         deal_scales(nc.gpsimd, w2_s, w2_s_raw, 0, PACK)
         og_w = tile("og_w", [P, J], U32, tag="xt_w")
@@ -205,19 +195,30 @@ def tile_list_boardssum_kernel(tc, xt_words, xt_scales, xo_words, xo_scales, w_w
                                 rhs=pa_w[:, ccols].bitcast(E4M3), rhs_scale=pa_s[:, ccols], start=True, stop=False)
             sums[(h, s)] = bank
 
-        b_woven = [tile(f"b_woven{h}", [P, HALF_C, PACK], BF16) for h in range(2)]
-        for t in range(PACK):
-            for h in range(2):
-                nc.vector.tensor_copy(b_woven[h][:, :, t], board_b[t][:, h * HALF_C : (h + 1) * HALF_C])
-        p_sb = [tile(f"p_sb{s}", [P, C], F32) for s in range(2)]
-        for h in range(2):
-            pb_w = tile(f"pb_w{h}", [P, HALF_C], U32)
-            pb_s = tile(f"pb_s{h}", [P, HALF_C], U8)
-            nc.vector.quantize_mx(out=pb_w[:].bitcast(E4M3), scales=pb_s[:], in_=b_woven[h][:].rearrange("p c t -> p (c t)"))
+        b_woven = [tile(f"b_woven{g}", [P, QUART_C, PACK], BF16) for g in range(4)]
+
+        def round_b(t, g):
+            nc.vector.tensor_copy(b_woven[g][:, :, t], board_b[t][:, g * QUART_C : (g + 1) * QUART_C])
+
+        def quantise_b(g):
+            pb_w = tile(f"pb_w{g}", [P, QUART_C], U32)
+            pb_s = tile(f"pb_s{g}", [P, QUART_C], U8)
+            nc.vector.quantize_mx(out=pb_w[:].bitcast(E4M3), scales=pb_s[:], in_=b_woven[g][:].rearrange("p c t -> p (c t)"))
             for s in range(2):
-                nc.tensor.matmul_mx(sums[(h, s)][:], lhsT=wc_w[:, 2 * s * P : 2 * (s + 1) * P].bitcast(E2M1),
+                nc.tensor.matmul_mx(sums[(g // 2, s)][:, (g % 2) * QUART_C : (g % 2 + 1) * QUART_C],
+                                    lhsT=wc_w[:, 2 * s * P : 2 * (s + 1) * P].bitcast(E2M1),
                                     lhsT_scale=wc_s[:, s * P : (s + 1) * P],
-                                    rhs=pb_w[:].bitcast(E4M3), rhs_scale=pb_s[:], start=False, stop=True)
+                                    rhs=pb_w[:].bitcast(E4M3), rhs_scale=pb_s[:], start=False, stop=(g % 2 == 1))
+
+        for t in range(PACK - 1):
+            for g in range(4):
+                round_b(t, g)
+        round_b(PACK - 1, 0)
+        for g in range(4):
+            if g + 1 < 4:
+                round_b(PACK - 1, g + 1)
+            quantise_b(g)
+        p_sb = [tile(f"p_sb{s}", [P, C], F32) for s in range(2)]
         for h in range(2):
             for s in range(2):
                 dst = p_sb[s][:, h * HALF_C : (h + 1) * HALF_C]
@@ -226,11 +227,12 @@ def tile_list_boardssum_kernel(tc, xt_words, xt_scales, xo_words, xo_scales, w_w
                 else:
                     nc.scalar.copy(dst, sums[(h, s)][:])
 
+        scaled = [tile(f"scaled{s}", [P, U], F32) for s in range(2)]
+        picked = [tile(f"picked{s}", [P, U], F32) for s in range(2)]
         for s in range(2):
-            scaled = tile(f"scaled{s}", [P, U], F32)
-            nc.scalar.activation(scaled[:], p_sb[s][:].indirect(l5[:]), COPY, scale=so_t[:, s : s + 1])
-            picked = tile(f"picked{s}", [P, U], F32)
-            nc.vector.tensor_copy(picked[:], p_sb[s][:].indirect(l6[:]))
+            nc.scalar.activation(scaled[s][:], p_sb[s][:].indirect(l5[:]), COPY, scale=so_t[:, s : s + 1])
+            nc.vector.tensor_copy(picked[s][:], p_sb[s][:].indirect(l6[:]))
+        for s in range(2):
             best = tile(f"best{s}", [P, U], F32)
-            nc.vector.tensor_tensor(best[:], scaled[:], picked[:], MAX)
+            nc.vector.tensor_tensor(best[:], scaled[s][:], picked[s][:], MAX)
             nc.sync.dma_start(out[s * P : (s + 1) * P, :], best[:])

@@ -20,10 +20,12 @@ MAX = mybir.AluOpType.max
 P = 128
 PACK = 4
 QUADS = 4
+SCALE_ROWS = 4
+PER_COLUMN = 16
 HALF_J = J // 2
-HALF_C = C // 2
-QUART_C = C // 4
-LIST_COLS = J // 16
+QUARTERS = 4
+QUART_C = C // QUARTERS
+N_TILES = N // P
 
 
 def tile_list_boardssum_kernel(tc, xt_words, xt_scales, xo_words, xo_scales, w_words, w_scales,
@@ -38,57 +40,58 @@ def tile_list_boardssum_kernel(tc, xt_words, xt_scales, xo_words, xo_scales, w_w
             return sb.tile(shape, dtype, name=name, tag=tag or name, align_bytes=64)
 
         def load_list(name, src):
-            t = sb.tile([P, LIST_COLS], U16, name=name)
-            nc.sync.dma_start(t[:], src)
-            return t
+            held = sb.tile([P, J // PER_COLUMN], U16, name=name)
+            nc.sync.dma_start(held[:], src)
+            return held
 
         def words_i32(src):
             return src[0].rearrange("p n t -> p (n t)").bitcast(I32)
 
         def stage_scales(name, src, width):
-            t = tile(name, [P, 2, width // 4], I32)
+            staged = tile(name, [P, 2, width // 4], I32)
             rows = src[0].bitcast(I32).rearrange("(g q r) c -> g r q c", g=2, q=2)
-            nc.sync.dma_start(t[0:QUADS, :, :], rows[0])
-            nc.scalar.dma_start(t[64 : 64 + QUADS, :, :], rows[1])
-            return t
+            nc.sync.dma_start(staged[0:SCALE_ROWS, :, :], rows[0])
+            nc.scalar.dma_start(staged[64 : 64 + SCALE_ROWS, :, :], rows[1])
+            return staged
 
         def spread_scales(plane, staged):
             for q in range(QUADS):
                 first = 64 * (q // 2)
-                nc.vector.tensor_copy(plane[32 * q : 32 * q + QUADS, :].bitcast(I32), staged[first : first + QUADS, q % 2, :])
+                nc.vector.tensor_copy(plane[32 * q : 32 * q + SCALE_ROWS, :].bitcast(I32),
+                                      staged[first : first + SCALE_ROWS, q % 2, :])
 
         def load_scales(plane, src):
             for q in range(QUADS):
-                nc.sync.dma_start(plane[32 * q : 32 * q + QUADS, :].bitcast(I32),
-                                  src[0, QUADS * q : QUADS * (q + 1), :].bitcast(I32))
+                nc.sync.dma_start(plane[32 * q : 32 * q + SCALE_ROWS, :].bitcast(I32),
+                                  src[0, SCALE_ROWS * q : SCALE_ROWS * (q + 1), :].bitcast(I32))
 
         def zero_plane(name, width):
-            t = tile(name, [P, width], U8)
-            nc.vector.memset(t[:].bitcast(I32), 0)
-            return t
+            plane = tile(name, [P, width], U8)
+            nc.vector.memset(plane[:].bitcast(I32), 0)
+            return plane
 
-        def zero_board(engine, name, tag=None):
-            t = tile(name, [P, C], F32, tag=tag)
-            engine.memset(t[:], 0.0)
-            return t
+        def zero_board(name, tag=None):
+            board = tile(name, [P, C], F32, tag=tag)
+            nc.vector.memset(board[:], 0.0)
+            return board
 
-        def deal_words(dst, src, t0, t1):
-            nc.vector.tensor_copy(dst[:].rearrange("p (t m) -> p m t", t=PACK)[:, :, t0:t1],
-                                  src[:].rearrange("p (m t) -> p m t", t=PACK)[:, :, t0:t1])
+        def deal_words(copy, dst, src, t0, t1):
+            copy(dst[:].rearrange("p (t m) -> p m t", t=PACK)[:, :, t0:t1],
+                 src[:].rearrange("p (m t) -> p m t", t=PACK)[:, :, t0:t1])
 
-        def deal_scales(engine, dst, src, t0, t1):
-            engine.tensor_copy(dst[:].rearrange("p (t m) -> p t m", t=PACK)[:, t0:t1, :],
-                               src[:].rearrange("p (m t) -> p t m", t=PACK)[:, t0:t1, :])
+        def deal_scales(dst, src, t0, t1):
+            nc.vector.tensor_copy(dst[:].rearrange("p (t m) -> p t m", t=PACK)[:, t0:t1, :],
+                                  src[:].rearrange("p (m t) -> p t m", t=PACK)[:, t0:t1, :])
 
-        l1 = load_list("l1", offs)
+        idx = load_list("idx", offs)
         xt_stage = stage_scales("xt_stage", xt_scales, T)
         w_stage = stage_scales("w_stage", w_scales, R)
         xt_w = tile("xt_w", [P, T], U16)
         nc.sync.dma_start(xt_w[:].bitcast(I32), xt_words[0].bitcast(I32))
         w_raw = tile("w_raw", [P, R], U32)
-        nc.sync.dma_start(w_raw[:].bitcast(I32), words_i32(w_words))
-        l3 = load_list("l3", offs3)
-        l2 = load_list("l2", offs2)
+        nc.scalar.dma_start(w_raw[:].bitcast(I32), words_i32(w_words))
+        idx3 = load_list("idx3", offs3)
+        idx2 = load_list("idx2", offs2)
         xo_w = tile("xo_w", [P, Z], U32)
         nc.sync.dma_start(xo_w[:].bitcast(I32), words_i32(xo_words))
         w2_raw = tile("w2_raw", [P, R], U32)
@@ -100,20 +103,21 @@ def tile_list_boardssum_kernel(tc, xt_words, xt_scales, xo_words, xo_scales, w_w
         w2_s_raw = zero_plane("w2_s_raw", R)
         wb_s = zero_plane("wb_s", N)
         wc_s = zero_plane("wc_s", N)
-        board_a = [zero_board(nc.vector if t < 2 else nc.gpsimd, f"board_a{t}") for t in range(PACK)]
+        board_a = [zero_board(f"board_a{t}") for t in range(PACK)]
+        board_b = [zero_board("board_b0")]
 
         load_scales(xo_s, xo_scales)
         load_scales(w2_s_raw, w2_scales)
-        l4 = load_list("l4", offs4)
+        idx4 = load_list("idx4", offs4)
         wb_w = tile("wb_w", [P, N], U32)
         nc.sync.dma_start(wb_w[:].bitcast(I32), words_i32(wb_words))
         load_scales(wb_s, wb_scales)
         wc_w = tile("wc_w", [P, 2 * N], U8)
         nc.sync.dma_start(wc_w[:].bitcast(I32), wc_words[0].bitcast(I32))
         load_scales(wc_s, wc_scales)
-        l5 = load_list("l5", offs5)
-        l6 = load_list("l6", offs6)
-        so_t = tile("so_t", [P, N // P], F32)
+        idx5 = load_list("idx5", offs5)
+        idx6 = load_list("idx6", offs6)
+        so_t = tile("so_t", [P, N_TILES], F32)
         with nc.allow_non_contiguous_dma(reason="one weight a partition"):
             nc.sync.dma_start(so_t[:], so.rearrange("(s p) o -> p (s o)", p=P))
 
@@ -125,114 +129,122 @@ def tile_list_boardssum_kernel(tc, xt_words, xt_scales, xo_words, xo_scales, w_w
         xg_s = tile("xg_s", [P, J], U8)
 
         def gather_xt(j0, j1):
-            nc.vector.tensor_copy(xg_s[:, j0:j1], xt_s[:].indirect(l1[:, j0 // 16 : j1 // 16]))
-            nc.vector.tensor_copy(xg_w[:, j0:j1], xt_w[:].indirect(l1[:, j0 // 16 : j1 // 16]))
+            entries = idx[:, j0 // PER_COLUMN : j1 // PER_COLUMN]
+            nc.vector.tensor_copy(xg_s[:, j0:j1], xt_s[:].indirect(entries))
+            nc.vector.tensor_copy(xg_w[:, j0:j1], xt_w[:].indirect(entries))
 
-        deal_scales(nc.vector, w_s, w_s_raw, 0, 1)
+        deal_scales(w_s, w_s_raw, 0, 1)
         gather_xt(0, HALF_J)
-        deal_words(w_w, w_raw, 0, 1)
-        deal_scales(nc.vector, w_s, w_s_raw, 1, PACK)
-        deal_words(w_w, w_raw, 1, PACK)
+        deal_words(nc.scalar.copy, w_w, w_raw, 0, 1)
+        deal_scales(w_s, w_s_raw, 1, PACK)
+        deal_words(nc.scalar.copy, w_w, w_raw, 1, PACK)
 
-        def products_a(ts, j0, j1, bank, on_scalar=False):
+        def vector_copy(dst, src):
+            nc.vector.tensor_copy(dst, src)
+
+        def scalar_copy(dst, src):
+            nc.scalar.activation(dst, src, COPY)
+
+        def products_a(ts, j0, j1, bank, copy_out):
             acc = ps.tile([P, len(ts), j1 - j0], F32, name=f"a_ps{bank}", tag=f"bank{bank}")
             for e, t in enumerate(ts):
                 cols = slice(t * P, (t + 1) * P)
                 nc.tensor.matmul_mx(acc[:, e, :], lhsT=w_w[:, cols].bitcast(E5M2), lhsT_scale=w_s[:, cols],
                                     rhs=xg_w[:, j0:j1].bitcast(E2M1), rhs_scale=xg_s[:, j0:j1], start=True, stop=True)
             staged = tile(f"a_sb{bank}", [P, len(ts), j1 - j0], F32)
-            if on_scalar:
-                nc.scalar.activation(staged[:], acc[:], COPY)
-            else:
-                nc.vector.tensor_copy(staged[:], acc[:])
+            copy_out(staged[:], acc[:])
             for e, t in enumerate(ts):
-                nc.scalar.activation(board_a[t][:].indirect(l3[:, j0 // 16 : j1 // 16]), staged[:, e, :], COPY)
+                entries = idx3[:, j0 // PER_COLUMN : j1 // PER_COLUMN]
+                nc.scalar.activation(board_a[t][:].indirect(entries), staged[:, e, :], COPY)
 
-        products_a([0], 0, HALF_J, 0, on_scalar=True)
-        products_a([1], 0, HALF_J, 5)
+        products_a([0], 0, HALF_J, 0, scalar_copy)
+        products_a([1], 0, HALF_J, 5, vector_copy)
         gather_xt(HALF_J, J)
-        products_a([2], 0, J, 1)
-        products_a([3], 0, J, 2)
-        products_a([0, 1], HALF_J, J, 6)
+        products_a([2], 0, J, 1, vector_copy)
+        products_a([3], 0, J, 2, vector_copy)
+        products_a([0, 1], HALF_J, J, 6, vector_copy)
 
-        board_b = [zero_board(nc.gpsimd, f"board_b{t}", tag=old) for t, old in enumerate(["w_raw", "w_s_raw", "xg_w", "xg_s"])]
-        w2_s = tile("w2_s", [P, R], U8, tag="w_s")
-        deal_scales(nc.gpsimd, w2_s, w2_s_raw, 0, PACK)
-        og_w = tile("og_w", [P, J], U32, tag="xt_w")
-        nc.vector.tensor_copy(og_w[:], xo_w[:].indirect(l2[:]))
-        og_s = tile("og_s", [P, J], U8, tag="xt_s")
-        nc.vector.tensor_copy(og_s[:], xo_s[:].indirect(l2[:]))
+        og_w = tile("og_w", [P, J], U32, tag="xg_w")
+        nc.vector.tensor_copy(og_w[:], xo_w[:].indirect(idx2[:]))
+        og_s = tile("og_s", [P, J], U8, tag="xg_s")
+        nc.vector.tensor_copy(og_s[:], xo_s[:].indirect(idx2[:]))
         w2_w = tile("w2_w", [P, R], U32, tag="w_w")
-        deal_words(w2_w, w2_raw, 0, PACK)
+        deal_words(nc.vector.tensor_copy, w2_w, w2_raw, 0, PACK)
+        w2_s = tile("w2_s", [P, R], U8, tag="w_s")
+        deal_scales(w2_s, w2_s_raw, 0, PACK)
         b_sb = []
-        for pair in range(2):
-            bank = ps.tile([P, 2, J], F32, name=f"b_ps{pair}", tag=f"bank{3 + pair}")
+        for pair in range(PACK // 2):
+            acc = ps.tile([P, 2, J], F32, name=f"b_ps{pair}", tag=f"bank{3 + pair}")
             for e in range(2):
                 cols = slice((2 * pair + e) * P, (2 * pair + e + 1) * P)
-                nc.tensor.matmul_mx(bank[:, e, :], lhsT=w2_w[:, cols].bitcast(E4M3), lhsT_scale=w2_s[:, cols],
+                nc.tensor.matmul_mx(acc[:, e, :], lhsT=w2_w[:, cols].bitcast(E4M3), lhsT_scale=w2_s[:, cols],
                                     rhs=og_w[:].bitcast(E5M2), rhs_scale=og_s[:], start=True, stop=True)
             staged = tile(f"b_sb{pair}", [P, 2, J], F32)
-            nc.vector.tensor_copy(staged[:], bank[:])
+            nc.vector.tensor_copy(staged[:], acc[:])
             b_sb.append(staged)
+        for t, finished in enumerate(["xg_w", "xg_s", "w_s"]):
+            board_b.append(zero_board(f"board_b{t + 1}", tag=finished))
         for t in range(PACK):
-            nc.scalar.activation(board_b[t][:].indirect(l4[:]), b_sb[t // 2][:, t % 2, :], COPY)
+            nc.scalar.activation(board_b[t][:].indirect(idx4[:]), b_sb[t // 2][:, t % 2, :], COPY)
 
-        a_planes = tile("a_planes", [P, PACK, C], BF16, tag="w_w")
+        a_rows = tile("a_rows", [P, PACK, C], BF16, tag="w_w")
         for t in range(PACK):
-            nc.vector.tensor_copy(a_planes[:, t, :], board_a[t][:])
+            nc.vector.tensor_copy(a_rows[:, t, :], board_a[t][:])
         a_woven = tile("a_woven", [P, C, PACK], BF16)
         nc.vector.tensor_copy(a_woven[:].rearrange("p (c i) t -> p c t i", i=4),
-                              a_planes[:].rearrange("p t (c i) -> p c t i", i=4))
+                              a_rows[:].rearrange("p t (c i) -> p c t i", i=4))
         pa_w = tile("pa_w", [P, C], U32)
         pa_s = tile("pa_s", [P, C], U8)
         nc.vector.quantize_mx(out=pa_w[:].bitcast(E4M3), scales=pa_s[:], in_=a_woven[:].rearrange("p c t -> p (c t)"))
         sums = {}
-        for k, (h, s) in enumerate([(h, s) for h in range(2) for s in range(2)]):
-            bank = ps.tile([P, HALF_C], F32, name=f"p_ps{h}{s}", tag=f"bank{(5 + k) % 8}")
-            ncols = slice(s * P, (s + 1) * P)
-            ccols = slice(h * HALF_C, (h + 1) * HALF_C)
-            nc.tensor.matmul_mx(bank[:], lhsT=wb_w[:, ncols].bitcast(E4M3), lhsT_scale=wb_s[:, ncols],
-                                rhs=pa_w[:, ccols].bitcast(E4M3), rhs_scale=pa_s[:, ccols], start=True, stop=False)
-            sums[(h, s)] = bank
+        for g in range(QUARTERS):
+            for s in range(N_TILES):
+                acc = ps.tile([P, QUART_C], F32, name=f"p_ps{g}{s}", tag=f"bank{N_TILES * g + s}")
+                ncols = slice(s * P, (s + 1) * P)
+                ccols = slice(g * QUART_C, (g + 1) * QUART_C)
+                nc.tensor.matmul_mx(acc[:], lhsT=wb_w[:, ncols].bitcast(E4M3), lhsT_scale=wb_s[:, ncols],
+                                    rhs=pa_w[:, ccols].bitcast(E4M3), rhs_scale=pa_s[:, ccols], start=True, stop=False)
+                sums[(g, s)] = acc
 
-        b_woven = [tile(f"b_woven{g}", [P, QUART_C, PACK], BF16) for g in range(4)]
+        b_woven = [tile(f"b_woven{g}", [P, QUART_C, PACK], BF16) for g in range(QUARTERS)]
 
         def round_b(t, g):
             nc.vector.tensor_copy(b_woven[g][:, :, t], board_b[t][:, g * QUART_C : (g + 1) * QUART_C])
 
-        def quantise_b(g):
+        def quantise_and_multiply_b(g):
             pb_w = tile(f"pb_w{g}", [P, QUART_C], U32)
             pb_s = tile(f"pb_s{g}", [P, QUART_C], U8)
             nc.vector.quantize_mx(out=pb_w[:].bitcast(E4M3), scales=pb_s[:], in_=b_woven[g][:].rearrange("p c t -> p (c t)"))
-            for s in range(2):
-                nc.tensor.matmul_mx(sums[(g // 2, s)][:, (g % 2) * QUART_C : (g % 2 + 1) * QUART_C],
+            for s in range(N_TILES):
+                nc.tensor.matmul_mx(sums[(g, s)][:],
                                     lhsT=wc_w[:, 2 * s * P : 2 * (s + 1) * P].bitcast(E2M1),
                                     lhsT_scale=wc_s[:, s * P : (s + 1) * P],
-                                    rhs=pb_w[:].bitcast(E4M3), rhs_scale=pb_s[:], start=False, stop=(g % 2 == 1))
+                                    rhs=pb_w[:].bitcast(E4M3), rhs_scale=pb_s[:], start=False, stop=True)
 
         for t in range(PACK - 1):
-            for g in range(4):
+            for g in range(QUARTERS):
                 round_b(t, g)
         round_b(PACK - 1, 0)
-        for g in range(4):
-            if g + 1 < 4:
+        for g in range(QUARTERS):
+            if g + 1 < QUARTERS:
                 round_b(PACK - 1, g + 1)
-            quantise_b(g)
-        p_sb = [tile(f"p_sb{s}", [P, C], F32) for s in range(2)]
-        for h in range(2):
-            for s in range(2):
-                dst = p_sb[s][:, h * HALF_C : (h + 1) * HALF_C]
-                if (h, s) == (1, 1):
-                    nc.vector.tensor_copy(dst, sums[(h, s)][:])
-                else:
-                    nc.scalar.copy(dst, sums[(h, s)][:])
+            quantise_and_multiply_b(g)
 
-        scaled = [tile(f"scaled{s}", [P, U], F32) for s in range(2)]
-        picked = [tile(f"picked{s}", [P, U], F32) for s in range(2)]
-        for s in range(2):
-            nc.scalar.activation(scaled[s][:], p_sb[s][:].indirect(l5[:]), COPY, scale=so_t[:, s : s + 1])
-            nc.vector.tensor_copy(picked[s][:], p_sb[s][:].indirect(l6[:]))
-        for s in range(2):
+        p_sb = [tile(f"p_sb{s}", [P, C], F32) for s in range(N_TILES)]
+        for g in range(QUARTERS):
+            for s in range(N_TILES):
+                dst = p_sb[s][:, g * QUART_C : (g + 1) * QUART_C]
+                if (g, s) == (QUARTERS - 1, 0):
+                    nc.vector.tensor_copy(dst, sums[(g, s)][:])
+                else:
+                    nc.scalar.copy(dst, sums[(g, s)][:])
+
+        scaled = [tile(f"scaled{s}", [P, U], F32) for s in range(N_TILES)]
+        picked = [tile(f"picked{s}", [P, U], F32) for s in range(N_TILES)]
+        for s in range(N_TILES):
+            nc.scalar.activation(scaled[s][:], p_sb[s][:].indirect(idx5[:]), COPY, scale=so_t[:, s : s + 1])
+            nc.vector.tensor_copy(picked[s][:], p_sb[s][:].indirect(idx6[:]))
+        for s in range(N_TILES):
             best = tile(f"best{s}", [P, U], F32)
             nc.vector.tensor_tensor(best[:], scaled[s][:], picked[s][:], MAX)
             nc.sync.dma_start(out[s * P : (s + 1) * P, :], best[:])

from contextlib import ExitStack

import concourse.mybir as mybir

K, T, J, R, F, Z, C, N, U = 512, 1024, 256, 512, 512, 1024, 512, 256, 256
FLOPS = 2 * K * R * J + 2 * F * R * J + 2 * 2 * R * N * C

F32 = mybir.dt.float32
BF16 = mybir.dt.bfloat16
I32 = mybir.dt.int32
U32 = mybir.dt.uint32
U16 = mybir.dt.uint16
U8 = mybir.dt.uint8
E4M3 = mybir.dt.float8_e4m3fn_x4
E5M2 = mybir.dt.float8_e5m2_x4
E2M1 = mybir.dt.float4_e2m1fn_x4
COPY = mybir.ActivationFunctionType.Copy
MAX = mybir.AluOpType.max

P = 128
PACK = 4
QUADS = 4
SCALE_ROWS = 4
PER_COLUMN = 16
HALF_J = J // 2
QUARTERS = 4
QUART_C = C // QUARTERS
N_TILES = N // P


def tile_list_boardssum_kernel(tc, xt_words, xt_scales, xo_words, xo_scales, w_words, w_scales,
                                     w2_words, w2_scales, wb_words, wb_scales, wc_words, wc_scales,
                                     so, offs, offs2, offs3, offs4, offs5, offs6, out):
    nc = tc.nc
    with ExitStack() as ctx:
        sb = ctx.enter_context(tc.tile_pool(name="sb", bufs=1))
        ps = ctx.enter_context(tc.psum_pool(name="ps", bufs=1))

        def tile(name, shape, dtype, tag=None):
            return sb.tile(shape, dtype, name=name, tag=tag or name, align_bytes=64)

        def load_list(name, src):
            held = sb.tile([P, J // PER_COLUMN], U16, name=name)
            nc.sync.dma_start(held[:], src)
            return held

        def words_i32(src):
            return src[0].rearrange("p n t -> p (n t)").bitcast(I32)

        def stage_scales(name, src, width):
            staged = tile(name, [P, 2, width // 4], I32)
            rows = src[0].bitcast(I32).rearrange("(g q r) c -> g r q c", g=2, q=2)
            nc.sync.dma_start(staged[0:SCALE_ROWS, :, :], rows[0])
            nc.scalar.dma_start(staged[64 : 64 + SCALE_ROWS, :, :], rows[1])
            return staged

        def spread_scales(plane, staged):
            for q in range(QUADS):
                first = 64 * (q // 2)
                nc.vector.tensor_copy(plane[32 * q : 32 * q + SCALE_ROWS, :].bitcast(I32),
                                      staged[first : first + SCALE_ROWS, q % 2, :])

        def load_scales(plane, src):
            for q in range(QUADS):
                nc.sync.dma_start(plane[32 * q : 32 * q + SCALE_ROWS, :].bitcast(I32),
                                  src[0, SCALE_ROWS * q : SCALE_ROWS * (q + 1), :].bitcast(I32))

        def zero_plane(name, width):
            plane = tile(name, [P, width], U8)
            nc.vector.memset(plane[:].bitcast(I32), 0)
            return plane

        def zero_board(name, tag=None):
            board = tile(name, [P, C], F32, tag=tag)
            nc.vector.memset(board[:], 0.0)
            return board

        def deal_words(copy, dst, src, t0, t1):
            copy(dst[:].rearrange("p (t m) -> p m t", t=PACK)[:, :, t0:t1],
                 src[:].rearrange("p (m t) -> p m t", t=PACK)[:, :, t0:t1])

        def deal_scales(dst, src, t0, t1):
            nc.vector.tensor_copy(dst[:].rearrange("p (t m) -> p t m", t=PACK)[:, t0:t1, :],
                                  src[:].rearrange("p (m t) -> p t m", t=PACK)[:, t0:t1, :])

        idx = load_list("idx", offs)
        xt_stage = stage_scales("xt_stage", xt_scales, T)
        w_stage = stage_scales("w_stage", w_scales, R)
        xt_w = tile("xt_w", [P, T], U16)
        nc.sync.dma_start(xt_w[:].bitcast(I32), xt_words[0].bitcast(I32))
        w_raw = tile("w_raw", [P, R], U32)
        nc.scalar.dma_start(w_raw[:].bitcast(I32), words_i32(w_words))
        idx3 = load_list("idx3", offs3)
        idx2 = load_list("idx2", offs2)
        xo_w = tile("xo_w", [P, Z], U32)
        nc.sync.dma_start(xo_w[:].bitcast(I32), words_i32(xo_words))
        w2_raw = tile("w2_raw", [P, R], U32)
        nc.sync.dma_start(w2_raw[:].bitcast(I32), words_i32(w2_words))

        xt_s = zero_plane("xt_s", T)
        w_s_raw = zero_plane("w_s_raw", R)
        xo_s = zero_plane("xo_s", Z)
        w2_s_raw = zero_plane("w2_s_raw", R)
        wb_s = zero_plane("wb_s", N)
        wc_s = zero_plane("wc_s", N)
        board_a = [zero_board(f"board_a{t}") for t in range(PACK)]
        board_b = [zero_board("board_b0")]

        load_scales(xo_s, xo_scales)
        load_scales(w2_s_raw, w2_scales)
        idx4 = load_list("idx4", offs4)
        wb_w = tile("wb_w", [P, N], U32)
        nc.sync.dma_start(wb_w[:].bitcast(I32), words_i32(wb_words))
        load_scales(wb_s, wb_scales)
        wc_w = tile("wc_w", [P, 2 * N], U8)
        nc.sync.dma_start(wc_w[:].bitcast(I32), wc_words[0].bitcast(I32))
        load_scales(wc_s, wc_scales)
        idx5 = load_list("idx5", offs5)
        idx6 = load_list("idx6", offs6)
        so_t = tile("so_t", [P, N_TILES], F32)
        with nc.allow_non_contiguous_dma(reason="one weight a partition"):
            nc.sync.dma_start(so_t[:], so.rearrange("(s p) o -> p (s o)", p=P))

        spread_scales(xt_s, xt_stage)
        spread_scales(w_s_raw, w_stage)
        w_s = tile("w_s", [P, R], U8)
        w_w = tile("w_w", [P, R], U32)
        xg_w = tile("xg_w", [P, J], U16)
        xg_s = tile("xg_s", [P, J], U8)

        def gather_xt(j0, j1):
            entries = idx[:, j0 // PER_COLUMN : j1 // PER_COLUMN]
            nc.vector.tensor_copy(xg_s[:, j0:j1], xt_s[:].indirect(entries))
            nc.vector.tensor_copy(xg_w[:, j0:j1], xt_w[:].indirect(entries))

        deal_scales(w_s, w_s_raw, 0, 1)
        gather_xt(0, HALF_J)
        deal_words(nc.scalar.copy, w_w, w_raw, 0, 1)
        deal_scales(w_s, w_s_raw, 1, PACK)
        deal_words(nc.scalar.copy, w_w, w_raw, 1, PACK)

        def vector_copy(dst, src):
            nc.vector.tensor_copy(dst, src)

        def scalar_copy(dst, src):
            nc.scalar.activation(dst, src, COPY)

        def products_a(ts, j0, j1, bank, copy_out):
            acc = ps.tile([P, len(ts), j1 - j0], F32, name=f"a_ps{bank}", tag=f"bank{bank}")
            for e, t in enumerate(ts):
                cols = slice(t * P, (t + 1) * P)
                nc.tensor.matmul_mx(acc[:, e, :], lhsT=w_w[:, cols].bitcast(E5M2), lhsT_scale=w_s[:, cols],
                                    rhs=xg_w[:, j0:j1].bitcast(E2M1), rhs_scale=xg_s[:, j0:j1], start=True, stop=True)
            staged = tile(f"a_sb{bank}", [P, len(ts), j1 - j0], F32)
            copy_out(staged[:], acc[:])
            for e, t in enumerate(ts):
                entries = idx3[:, j0 // PER_COLUMN : j1 // PER_COLUMN]
                nc.scalar.activation(board_a[t][:].indirect(entries), staged[:, e, :], COPY)

        products_a([0], 0, HALF_J, 0, scalar_copy)
        products_a([1], 0, HALF_J, 5, vector_copy)
        gather_xt(HALF_J, J)
        products_a([2], 0, J, 1, vector_copy)
        products_a([3], 0, J, 2, vector_copy)
        products_a([0, 1], HALF_J, J, 6, vector_copy)

        og_w = tile("og_w", [P, J], U32, tag="xg_w")
        nc.vector.tensor_copy(og_w[:], xo_w[:].indirect(idx2[:]))
        og_s = tile("og_s", [P, J], U8, tag="xg_s")
        nc.vector.tensor_copy(og_s[:], xo_s[:].indirect(idx2[:]))
        w2_w = tile("w2_w", [P, R], U32, tag="w_w")
        deal_words(nc.vector.tensor_copy, w2_w, w2_raw, 0, PACK)
        w2_s = tile("w2_s", [P, R], U8, tag="w_s")
        deal_scales(w2_s, w2_s_raw, 0, PACK)
        b_sb = []
        for pair in range(PACK // 2):
            acc = ps.tile([P, 2, J], F32, name=f"b_ps{pair}", tag=f"bank{3 + pair}")
            for e in range(2):
                cols = slice((2 * pair + e) * P, (2 * pair + e + 1) * P)
                nc.tensor.matmul_mx(acc[:, e, :], lhsT=w2_w[:, cols].bitcast(E4M3), lhsT_scale=w2_s[:, cols],
                                    rhs=og_w[:].bitcast(E5M2), rhs_scale=og_s[:], start=True, stop=True)
            staged = tile(f"b_sb{pair}", [P, 2, J], F32)
            nc.vector.tensor_copy(staged[:], acc[:])
            b_sb.append(staged)
        for t, finished in enumerate(["xg_w", "xg_s", "w_s"]):
            board_b.append(zero_board(f"board_b{t + 1}", tag=finished))
        for t in range(PACK):
            nc.scalar.activation(board_b[t][:].indirect(idx4[:]), b_sb[t // 2][:, t % 2, :], COPY)

        a_rows = tile("a_rows", [P, PACK, C], BF16, tag="w_w")
        for t in range(PACK):
            nc.vector.tensor_copy(a_rows[:, t, :], board_a[t][:])
        a_woven = tile("a_woven", [P, C, PACK], BF16)
        nc.vector.tensor_copy(a_woven[:].rearrange("p (c i) t -> p c t i", i=4),
                              a_rows[:].rearrange("p t (c i) -> p c t i", i=4))
        pa_w = tile("pa_w", [P, C], U32)
        pa_s = tile("pa_s", [P, C], U8)
        nc.vector.quantize_mx(out=pa_w[:].bitcast(E4M3), scales=pa_s[:], in_=a_woven[:].rearrange("p c t -> p (c t)"))
        sums = {}
        for g in range(QUARTERS):
            for s in range(N_TILES):
                acc = ps.tile([P, QUART_C], F32, name=f"p_ps{g}{s}", tag=f"bank{N_TILES * g + s}")
                ncols = slice(s * P, (s + 1) * P)
                ccols = slice(g * QUART_C, (g + 1) * QUART_C)
                nc.tensor.matmul_mx(acc[:], lhsT=wb_w[:, ncols].bitcast(E4M3), lhsT_scale=wb_s[:, ncols],
                                    rhs=pa_w[:, ccols].bitcast(E4M3), rhs_scale=pa_s[:, ccols], start=True, stop=False)
                sums[(g, s)] = acc

        b_woven = [tile(f"b_woven{g}", [P, QUART_C, PACK], BF16) for g in range(QUARTERS)]

        def round_b(t, g):
            nc.vector.tensor_copy(b_woven[g][:, :, t], board_b[t][:, g * QUART_C : (g + 1) * QUART_C])

        def quantise_and_multiply_b(g):
            pb_w = tile(f"pb_w{g}", [P, QUART_C], U32)
            pb_s = tile(f"pb_s{g}", [P, QUART_C], U8)
            nc.vector.quantize_mx(out=pb_w[:].bitcast(E4M3), scales=pb_s[:], in_=b_woven[g][:].rearrange("p c t -> p (c t)"))
            for s in range(N_TILES):
                nc.tensor.matmul_mx(sums[(g, s)][:],
                                    lhsT=wc_w[:, 2 * s * P : 2 * (s + 1) * P].bitcast(E2M1),
                                    lhsT_scale=wc_s[:, s * P : (s + 1) * P],
                                    rhs=pb_w[:].bitcast(E4M3), rhs_scale=pb_s[:], start=False, stop=True)

        for t in range(PACK - 1):
            for g in range(QUARTERS):
                round_b(t, g)
        round_b(PACK - 1, 0)
        for g in range(QUARTERS):
            if g + 1 < QUARTERS:
                round_b(PACK - 1, g + 1)
            quantise_and_multiply_b(g)

        p_sb = [tile(f"p_sb{s}", [P, C], F32) for s in range(N_TILES)]
        for g in range(QUARTERS):
            for s in range(N_TILES):
                dst = p_sb[s][:, g * QUART_C : (g + 1) * QUART_C]
                if (g, s) == (QUARTERS - 1, 0):
                    nc.vector.tensor_copy(dst, sums[(g, s)][:])
                else:
                    nc.scalar.copy(dst, sums[(g, s)][:])

        scaled = [tile(f"scaled{s}", [P, U], F32) for s in range(N_TILES)]
        picked = [tile(f"picked{s}", [P, U], F32) for s in range(N_TILES)]
        for s in range(N_TILES):
            nc.scalar.activation(scaled[s][:], p_sb[s][:].indirect(idx5[:]), COPY, scale=so_t[:, s : s + 1])
            nc.vector.tensor_copy(picked[s][:], p_sb[s][:].indirect(idx6[:]))
        for s in range(N_TILES):
            best = tile(f"best{s}", [P, U], F32)
            nc.vector.tensor_tensor(best[:], scaled[s][:], picked[s][:], MAX)
            nc.sync.dma_start(out[s * P : (s + 1) * P, :], best[:])
